import numpy as np
import ml_dtypes


def mxq(x, axis, fmt="e4m3"):
    dtype, down = {"e4m3": (ml_dtypes.float8_e4m3fn, 7), "e5m2": (ml_dtypes.float8_e5m2, 14)}[fmt]
    v = np.moveaxis(np.asarray(x, np.float32).astype(ml_dtypes.bfloat16).astype(np.float64), axis, -1)
    blocks = v.reshape(v.shape[:-1] + (-1, 32))
    amax = np.abs(blocks).max(-1, keepdims=True)
    byte = np.maximum(np.where(amax > 0, np.frexp(amax)[1] - 1 + 127, 0) - down, 1)
    scale = np.exp2(byte - 127.0)
    codes = (blocks / scale).astype(np.float32).astype(dtype).astype(np.float64)
    return np.moveaxis((codes * scale).reshape(v.shape), -1, axis)


WIDE = False


def mx_kscale(k):
    if not WIDE:
        return np.ones(k)
    levels = np.array([10, -10, 5, -5, 0])
    if k % 512:
        return np.exp2(np.random.permutation(np.resize(levels, k // 32))).repeat(32)
    a = np.empty((k // 512, 16))
    for p in range(k // 512):
        a[p, :8] = np.random.permutation(np.resize(levels, 8))
        for g in range(8):
            far = levels[np.abs(levels - a[p, g]) >= 10]
            a[p, g + 8] = far[np.random.randint(len(far))]
    return np.exp2(a.ravel()).repeat(32)


BF16 = ml_dtypes.bfloat16


def bf(x):
    return np.asarray(x, np.float32).astype(BF16)


def f64(x):
    return np.asarray(x).astype(np.float64)


E2M1 = np.array([0.0, 0.5, 1.0, 1.5, 2.0, 3.0, 4.0, 6.0, -0.0, -0.5, -1.0, -1.5, -2.0, -3.0, -4.0, -6.0])


def pack_weight(w, fmt):
    k, n = w.shape
    w = f64(bf(w)).reshape(k // 32, 32, n)
    amax = np.abs(w).max(1)
    if fmt == "e4m3":
        byte = np.frexp(amax)[1] - 1 + 127 - 7
    else:
        mant, ex = np.frexp(amax / 6.0)
        byte = np.where(mant > 0.5, ex, ex - 1) + 127
    byte = np.clip(np.where(amax > 0, byte, 1), 1, 254)
    scaled = (w * np.exp2(127.0 - byte)[:, None, :]).reshape(k, n).astype(np.float32)
    by_word = np.ascontiguousarray(scaled.reshape(k // 512, 128, 4, n).transpose(0, 1, 3, 2))
    if fmt == "e4m3":
        words = by_word.astype(ml_dtypes.float8_e4m3fn).view(np.uint8)
    else:
        c = by_word.astype(ml_dtypes.float4_e2m1fn).view(np.uint8) & 0xF
        words = c[..., 0::2] | (c[..., 1::2] << 4)
    return np.ascontiguousarray(words), np.ascontiguousarray(byte.astype(np.uint8).reshape(k // 512, 16, n))


def unpack_weight(words, scales, fmt):
    g, p, n, _ = words.shape
    if fmt == "e4m3":
        vals = np.ascontiguousarray(words).view(ml_dtypes.float8_e4m3fn).astype(np.float64)
    else:
        nib = np.empty((g, p, n, 4), np.uint8)
        nib[..., 0::2] = words & 0xF
        nib[..., 1::2] = words >> 4
        vals = E2M1[nib]
    vals = vals * np.repeat(np.exp2(scales.astype(np.float64) - 127.0), 8, axis=1)[..., None]
    return vals.transpose(0, 1, 3, 2).reshape(g * 512, n)
def pack4(w):
    words, scales = pack_weight(w, "e2m1")
    return words.reshape(words.shape[0], 128, -1), scales


def unpack4(words, scales):
    return unpack_weight(words.reshape(words.shape[0], 128, -1, 2), scales, "e2m1")


B, E, D, S = 1024, 1024, 512, 2048


def draw0():
    s, u, t = mx_kscale(E), mx_kscale(D), mx_kscale(S)
    counts = np.random.randint(-3, 4, (E, S)).astype(np.float64)
    mass = np.random.uniform(0.5, 1.5, E)
    f_words, f_scales = pack4(counts / (2 * np.sqrt(E)) / s[:, None])
    a_words, a_scales = pack4(counts.T * mass / (2 * np.sqrt(S)) / t[:, None])
    return {"lam": bf(0.6 * np.random.standard_normal((B, E)) * s),
            "f_words": f_words, "f_scales": f_scales,
            "phi": bf(0.5 * np.random.standard_normal((B, D)) * u),
            "g": bf(np.random.standard_normal((D, S)) / np.sqrt(D) / u[:, None]),
            "m": bf(np.random.uniform(0.5, 1.5, S) * t),
            "a_words": a_words, "a_scales": a_scales,
            "feed": bf(np.random.standard_normal((B, E)))}


def core(lam, f_words, f_scales, phi, g, m, a_words, a_scales, feed):
    F = unpack4(f_words, f_scales)
    A = unpack4(a_words, a_scales)
    z = (mxq(f64(lam), 1, "e4m3") @ F) + (mxq(f64(phi), 1, "e4m3") @ mxq(f64(g), 0, "e4m3"))
    n = np.exp(z) * f64(m)
    return (mxq(n, 1, "e4m3") @ A) - f64(feed)


def e4m3fn_bytes(y):
    return np.clip(np.asarray(y, np.float64), -448.0, 448.0).astype(np.float32).astype(ml_dtypes.float8_e4m3fn).view(np.uint8)


def e4m3fn_values(b):
    return np.asarray(b, np.uint8).view(ml_dtypes.float8_e4m3fn).astype(np.float64)


def setup_inputs():
    d = draw0()
    x0 = np.asarray(d['lam']).astype(np.float64)
    s = (np.max(np.abs(x0), axis=(0,), keepdims=True) / 448.0).astype(np.float32)
    out = {}
    for k, v in d.items():
        if k == 'lam':
            out['lam_bytes'] = e4m3fn_bytes(x0 / s.astype(np.float64))
            out['lam_scale'] = s
        else:
            out[k] = v
    return out


def reference(lam_bytes, lam_scale, f_words, f_scales, phi, g, m, a_words, a_scales, feed):
    return core(e4m3fn_values(lam_bytes) * lam_scale.astype(np.float64), f_words, f_scales, phi, g, m, a_words, a_scales, feed)

@@ -1,0 +1,381 @@
+from contextlib import ExitStack
+
+import concourse.mybir as mybir
+from concourse.masks import make_identity
+
+B, E, D, S = 1024, 1024, 512, 2048
+FLOPS = 2 * B * S * (E + D) + 2 * B * S * E
+
+F32 = mybir.dt.float32
+BF16 = mybir.dt.bfloat16
+U32 = mybir.dt.uint32
+I32 = mybir.dt.int32
+U8 = mybir.dt.uint8
+FP8 = mybir.dt.float8_e4m3fn
+FP8X4 = mybir.dt.float8_e4m3fn_x4
+FP4X4 = mybir.dt.float4_e2m1fn_x4
+ALU = mybir.AluOpType
+ACT = mybir.ActivationFunctionType
+
+P = 128
+HALF = 512
+ROWS = 4
+UNITS = S // 512
+LG = E // 512
+SCALED = {(1, 0), (1, 1), (1, 2)}
+
+
+def tile_equilibrium_mass_balance_s3_kernel(
+    tc, lam_bytes, lam_scale, f_words, f_scales, phi, g, m, a_words, a_scales, feed, out
+):
+    nc = tc.nc
+    with ExitStack() as ctx:
+        keep = ctx.enter_context(tc.tile_pool(name="keep", bufs=1))
+        work = ctx.enter_context(tc.tile_pool(name="work", bufs=2))
+        psum = ctx.enter_context(tc.psum_pool(name="psum", bufs=1))
+
+        lam_v = lam_bytes.rearrange("(h p c) k -> h p c k", h=2, c=ROWS)
+        phi_v = phi.rearrange("(h p c) k -> h p c k", h=2, c=ROWS)
+        feed_v = feed.rearrange("(h p c) e -> h p c e", h=2, c=ROWS)
+        out_v = out.rearrange("(h p c) e -> h p c e", h=2, c=ROWS)
+        g_v = g.rearrange("(p j) s -> p j s", j=4)
+        f_v = f_words.rearrange("k p b -> p k b")
+        a_v = a_words.rearrange("k p b -> p k b")
+
+        ident = keep.tile([P, P], F32, name="ident")
+        f_sc_raw = keep.tile([P, LG, S], U8, name="f_sc_raw", align_bytes=64)
+        nc.vector.memset(f_sc_raw[:].bitcast(I32), 0)
+        make_identity(nc, ident[:])
+        a_sc = keep.tile([P, UNITS, E], U8, name="a_sc", align_bytes=64)
+        nc.gpsimd.memset(a_sc[:].bitcast(I32), 0)
+        warm = keep.tile([P, 1], F32, name="warm")
+        nc.vector.memset(warm[:], 0.0)
+        nc.scalar.activation(warm[:], warm[:], ACT.Exp)
+
+        lam_sb, phi_sb, feed_sb = {}, {}, {}
+
+        def load_lam(h, cs):
+            if h not in lam_sb:
+                lam_sb[h] = keep.tile([P, ROWS, E], U8, name="lam_sb%d" % h)
+            nc.sync.dma_start(out=lam_sb[h][:, cs, :], in_=lam_v[h][:, cs, :])
+
+        def load_phi(h):
+            phi_sb[h] = keep.tile([P, ROWS, D], BF16, name="phi_sb%d" % h)
+            nc.sync.dma_start(out=phi_sb[h][:], in_=phi_v[h])
+
+        g_sb, f_sb = {}, {}
+
+        def load_g(u):
+            g_sb[u] = work.tile([P, 4, 512], BF16, name="g_sb", tag="g_sb", bufs=3)
+            nc.sync.dma_start(out=g_sb[u][:], in_=g_v[:, :, 512 * u : 512 * (u + 1)])
+
+        def load_f(u):
+            f_sb[u] = work.tile([P, LG, 1024], U8, name="f_sb", tag="f_sb", bufs=3)
+            nc.sync.dma_start(out=f_sb[u][:], in_=f_v[:, :, 1024 * u : 1024 * (u + 1)])
+
+        a_sb = keep.tile([P, UNITS, 2 * E], U8, name="a_sb", align_bytes=64)
+
+        def load_a(us):
+            nc.sync.dma_start(out=a_sb[:, us, :], in_=a_v[:, us, :])
+
+        def load_scales(dst, src):
+            rows = src.bitcast(I32).rearrange("k (q r) n -> r q k n", r=4)
+            words = dst[:].bitcast(I32)
+            for r in range(4):
+                nc.sync.dma_start(out=words[r:P:32], in_=rows[r])
+
+        load_f(0)
+        load_scales(f_sc_raw, f_scales)
+        scale_b = keep.tile([P, E], F32, name="scale_b")
+        nc.sync.dma_start(out=scale_b[:], in_=lam_scale.rearrange("o k -> (o k)").partition_broadcast(P))
+        load_lam(0, slice(0, 2))
+        load_phi(0)
+        load_g(0)
+        load_lam(0, slice(2, 4))
+        load_f(1)
+        load_g(1)
+        load_phi(1)
+        m_sb = keep.tile([P, UNITS, 4], BF16, name="m_sb")
+        nc.sync.dma_start(out=m_sb[:], in_=m.rearrange("(u p t) -> p u t", p=P, t=4))
+        m_f = keep.tile([P, UNITS * 4], F32, name="m_f")
+        nc.gpsimd.tensor_copy(out=m_f[:], in_=m_sb[:].rearrange("p u t -> p (u t)"))
+        load_f(2)
+        load_g(2)
+        load_f(3)
+        load_g(3)
+        load_lam(1, slice(0, 4))
+        load_scales(a_sc, a_scales)
+        load_a(slice(0, 2))
+        load_a(slice(2, 4))
+        for h in range(2):
+            feed_sb[h] = keep.tile([P, ROWS, E], BF16, name="feed_sb%d" % h)
+            nc.sync.dma_start(out=feed_sb[h][:], in_=feed_v[h])
+
+        phi_q, phi_s, lam_q, lam_s = {}, {}, {}, {}
+        phi_t, lam_t = {}, {}
+
+        def prep_phi(h, pair, tag):
+            if pair == 0:
+                phi_t[h] = work.tile([P, HALF, 4], BF16, name="phi_t", tag="phi_t", bufs=1, align_bytes=64)
+                phi_q[h] = keep.tile([P, HALF], U32, name="phi_q%d" % h, align_bytes=64)
+                phi_s[h] = keep.tile([P, HALF], U8, name="phi_s%d" % h, align_bytes=64)
+            tp = psum.tile([P, 512], F32, name="tp", tag=tag[0], bufs=tag[1])
+            for i in range(2):
+                words = phi_sb[h][:, 2 * pair + i, :].bitcast(F32)
+                for u in range(2):
+                    k = 128 * (2 * i + u)
+                    nc.tensor.transpose(tp[:, k : k + 128], words[:, u::2], ident[:])
+            dst = phi_t[h][:].rearrange("p r t -> p (r t)").bitcast(F32)
+            dst = dst.rearrange("p (c r u) -> p c r u", c=4, u=2)
+            nc.scalar.copy(dst[:, 2 * pair : 2 * pair + 2], tp[:].rearrange("p (c u r) -> p c r u", c=2, u=2))
+            if pair == 0:
+                return
+            cols = slice(0, HALF)
+            nc.vector.quantize_mx(
+                out=phi_q[h][:, cols].bitcast(FP8X4),
+                scales=phi_s[h][:, cols],
+                in_=phi_t[h][:, cols, :].rearrange("p r t -> p (r t)"),
+            )
+
+        def prep_lam(h, c, tag):
+            if c == 0:
+                lam_t[h] = work.tile([P, LG, HALF, 4], BF16, name="lam_t", tag="lam_t", bufs=1, align_bytes=64)
+                lam_q[h] = keep.tile([P, LG, HALF], U32, name="lam_q%d" % h, align_bytes=64)
+                lam_s[h] = keep.tile([P, LG, HALF], U8, name="lam_s%d" % h, align_bytes=64)
+            wide = work.tile([P, E], BF16, name="wide", tag="wide", bufs=3)
+            nc.vector.tensor_tensor(
+                out=wide[:], in0=lam_sb[h][:, c, :].bitcast(FP8), in1=scale_b[:], op=ALU.mult
+            )
+            words = wide[:].bitcast(F32)
+            tp = psum.tile([P, 512], F32, name="tp", tag=tag[0], bufs=tag[1])
+            for gg in range(LG):
+                for u in range(2):
+                    k = 128 * (2 * gg + u)
+                    nc.tensor.transpose(
+                        tp[:, k : k + 128], words[:, 256 * gg + u : 256 * (gg + 1) : 2], ident[:]
+                    )
+            dst = lam_t[h][:].rearrange("p g r t -> p (g r t)").bitcast(F32)
+            dst = dst.rearrange("p (g r u) -> p g r u", g=LG, u=2)
+            nc.scalar.copy(
+                dst[:, :, 128 * c : 128 * (c + 1), :], tp[:].rearrange("p (g u r) -> p g r u", g=LG, u=2)
+            )
+            n = 1 if h == 0 else 4
+            if c % n == n - 1:
+                cols = slice(128 * (c + 1 - n), 128 * (c + 1))
+                for gg in range(LG):
+                    nc.vector.quantize_mx(
+                        out=lam_q[h][:, gg, cols].bitcast(FP8X4),
+                        scales=lam_s[h][:, gg, cols],
+                        in_=lam_t[h][:, gg, cols, :].rearrange("p r t -> p (r t)"),
+                    )
+
+        g_q, g_s, f_p, f_sp = {}, {}, {}, {}
+
+        def prep_g(u):
+            gi = work.tile([P, 512, 4], BF16, name="gi", tag="gi", bufs=2, align_bytes=64)
+            for i in range(2):
+                ts = slice(2 * i, 2 * i + 2)
+                nc.scalar.copy(
+                    gi[:].rearrange("p (t m) j -> p t m j", t=4)[:, ts],
+                    g_sb[u][:].rearrange("p j (m t) -> p t m j", t=4)[:, ts],
+                )
+            g_q[u] = keep.tile([P, 512], U32, name="g_q%d" % u, align_bytes=64)
+            g_s[u] = keep.tile([P, 512], U8, name="g_s%d" % u, align_bytes=64)
+            nc.vector.quantize_mx(
+                out=g_q[u][:].bitcast(FP8X4), scales=g_s[u][:], in_=gi[:].rearrange("p s j -> p (s j)")
+            )
+
+        def prep_f(u):
+            f_p[u] = keep.tile([P, LG, 1024], U8, name="f_p%d" % u, align_bytes=64)
+            f_sp[u] = keep.tile([P, LG, 512], U8, name="f_sp%d" % u, align_bytes=64)
+            nc.vector.tensor_copy(
+                out=f_sp[u][:].rearrange("p k (t m) -> p k t m", t=4),
+                in_=f_sc_raw[:, :, 512 * u : 512 * (u + 1)].rearrange("p k (m t) -> p k t m", t=4),
+            )
+            for k in range(LG):
+                nc.vector.tensor_copy(
+                    out=f_p[u][:, k, :].rearrange("p (t m b) -> p t m b", t=4, b=2),
+                    in_=f_sb[u][:, k, :].rearrange("p (m t b) -> p t m b", t=4, b=2),
+                )
+
+        e_sb, n_q, n_s = {}, {}, {}
+
+        def z_passes(h, u, t, cells, dst):
+            cols = slice(128 * t, 128 * (t + 1))
+            nc.tensor.matmul_mx(
+                out=dst, lhsT=g_q[u][:, cols].bitcast(FP8X4), lhsT_scale=g_s[u][:, cols],
+                rhs=phi_q[h][:, cells].bitcast(FP8X4), rhs_scale=phi_s[h][:, cells], start=True, stop=False,
+            )
+            for k in range(LG):
+                nc.tensor.matmul_mx(
+                    out=dst,
+                    lhsT=f_p[u][:, k, 256 * t : 256 * (t + 1)].bitcast(FP4X4),
+                    lhsT_scale=f_sp[u][:, k, cols],
+                    rhs=lam_q[h][:, k, cells].bitcast(FP8X4),
+                    rhs_scale=lam_s[h][:, k, cells],
+                    start=False, stop=(k == LG - 1),
+                )
+
+        def new_e(h, u):
+            e_sb[h, u] = work.tile([P, 4, HALF], F32, name="e_sb", tag="e_sb", bufs=4)
+
+        def z_unit(h, u):
+            new_e(h, u)
+            for t in range(4):
+                zp = psum.tile([P, HALF], F32, name="zp", tag="z", bufs=3)
+                z_passes(h, u, t, slice(0, HALF), zp[:])
+                nc.scalar.activation(e_sb[h, u][:, t, :], zp[:], ACT.Exp)
+
+        def z_first(h, u):
+            new_e(h, u)
+            zps = [
+                psum.tile([P, HALF], F32, name="zp", tag=tag, bufs=n)
+                for tag, n in (("z", 3), ("z", 3), ("z", 3), ("x", 1))
+            ]
+            for c in range(4):
+                for t in range(4):
+                    cells = slice(128 * c, 128 * (c + 1))
+                    z_passes(h, u, t, cells, zps[t][:, cells])
+            for t in range(4):
+                nc.scalar.activation(e_sb[h, u][:, t, :], zps[t][:], ACT.Exp)
+
+        def z_last(h, u, c):
+            if c == 0:
+                new_e(h, u)
+            zp = psum.tile([P, HALF], F32, name="zp", tag="z", bufs=3)
+            cells = slice(128 * c, 128 * (c + 1))
+            for t in range(4):
+                z_passes(h, u, t, cells, zp[:, 128 * t : 128 * (t + 1)])
+            nc.scalar.activation(e_sb[h, u][:, :, cells], zp[:].rearrange("p (t r) -> p t r", t=4), ACT.Exp)
+
+        nb = {}
+
+        def amounts_s(h, u):
+            nb[h, u] = work.tile([P, HALF, 4], BF16, name="nb", tag="nb", bufs=3, align_bytes=64)
+            n_q[h, u] = keep.tile([P, HALF], U32, name="n_q%d%d" % (h, u), align_bytes=64)
+            n_s[h, u] = keep.tile([P, HALF], U8, name="n_s%d%d" % (h, u), align_bytes=64)
+            flat = work.tile([P, 4, HALF], BF16, name="flat", tag="flat", bufs=2)
+            for t in range(4):
+                nc.scalar.activation(
+                    flat[:, t, :], e_sb[h, u][:, t, :], ACT.Copy, scale=m_f[:, 4 * u + t : 4 * u + t + 1]
+                )
+            for cols in halves:
+                nc.vector.tensor_copy(
+                    out=nb[h, u][:, cols, :], in_=flat[:, :, cols].rearrange("p t r -> p r t")
+                )
+            for cols in halves:
+                nc.vector.quantize_mx(
+                    out=n_q[h, u][:, cols].bitcast(FP8X4),
+                    scales=n_s[h, u][:, cols],
+                    in_=nb[h, u][:, cols, :].rearrange("p r t -> p (r t)"),
+                )
+
+        def amounts(h, u, chunks):
+            if (h, u) in SCALED:
+                amounts_s(h, u)
+                return
+            if chunks[0].start == 0:
+                nb[h, u] = work.tile([P, HALF, 4], BF16, name="nb", tag="nb", bufs=3, align_bytes=64)
+                n_q[h, u] = keep.tile([P, HALF], U32, name="n_q%d%d" % (h, u), align_bytes=64)
+                n_s[h, u] = keep.tile([P, HALF], U8, name="n_s%d%d" % (h, u), align_bytes=64)
+            for cols in chunks:
+                nc.vector.tensor_tensor(
+                    out=nb[h, u][:, cols, :],
+                    in0=e_sb[h, u][:, :, cols].rearrange("p t r -> p r t"),
+                    in1=m_sb[:, u, :].unsqueeze(1).to_broadcast([P, cols.stop - cols.start, 4]),
+                    op=ALU.mult,
+                )
+            for cols in chunks:
+                nc.vector.quantize_mx(
+                    out=n_q[h, u][:, cols].bitcast(FP8X4),
+                    scales=n_s[h, u][:, cols],
+                    in_=nb[h, u][:, cols, :].rearrange("p r t -> p (r t)"),
+                )
+
+        acc = {}
+
+        def balance(h, u, e, cs):
+            for c in cs:
+                if (h, c, e) not in acc:
+                    if e == 0:
+                        tag = ("acc", 4)
+                    elif h == 0:
+                        tag = ("x", 1)
+                    else:
+                        tag = (("x", 1), ("z", 3), ("z", 3), ("z", 3))[c]
+                    acc[h, c, e] = psum.tile([P, 512], F32, name="ac", tag=tag[0], bufs=tag[1])
+                cols = slice(128 * c, 128 * (c + 1))
+                nc.tensor.matmul_mx(
+                    out=acc[h, c, e][:],
+                    lhsT=n_q[h, u][:, cols].bitcast(FP8X4), lhsT_scale=n_s[h, u][:, cols],
+                    rhs=a_sb[:, u, 1024 * e : 1024 * (e + 1)].bitcast(FP4X4),
+                    rhs_scale=a_sc[:, u, 512 * e : 512 * (e + 1)],
+                    start=(u == 0), stop=(u == UNITS - 1),
+                )
+
+        def finish(h, c, e):
+            o = work.tile([P, 512], F32, name="o", tag="o", bufs=10)
+            nc.vector.tensor_tensor(
+                out=o[:], in0=acc[h, c, e][:], in1=feed_sb[h][:, c, 512 * e : 512 * (e + 1)], op=ALU.subtract
+            )
+            nc.sync.dma_start(out=out_v[h][:, c, 512 * e : 512 * (e + 1)], in_=o[:])
+
+        allc = range(4)
+        halves = [slice(0, 256), slice(256, 512)]
+        prep_f(0)
+        prep_lam(0, 0, ("acc", 4))
+        prep_lam(0, 1, ("acc", 4))
+        prep_phi(0, 0, ("acc", 4))
+        prep_phi(0, 1, ("acc", 4))
+        prep_lam(0, 2, ("acc", 4))
+        prep_lam(0, 3, ("acc", 4))
+        prep_g(0)
+        prep_phi(1, 0, ("acc", 4))
+        prep_phi(1, 1, ("acc", 4))
+        z_first(0, 0)
+        for u in range(1, UNITS):
+            prep_f(u)
+            prep_g(u)
+            z_unit(0, u)
+        for i in range(2):
+            prep_lam(1, 2 * i, ("acc", 4))
+            prep_lam(1, 2 * i + 1, ("acc", 4))
+        amounts(0, 0, halves)
+        z_unit(1, 0)
+        amounts(0, 1, halves)
+        balance(0, 0, 0, allc)
+        amounts(0, 2, halves)
+        balance(0, 1, 0, allc)
+        z_unit(1, 1)
+        amounts(0, 3, halves)
+        balance(0, 2, 0, allc)
+        amounts(1, 0, halves)
+        balance(0, 3, 0, allc)
+        for c in allc:
+            finish(0, c, 0)
+        z_unit(1, 2)
+        for c in (0, 1):
+            for u in range(UNITS):
+                balance(0, u, 1, (c,))
+            finish(0, c, 1)
+        balance(1, 0, 0, allc)
+        amounts(1, 1, halves)
+        z_last(1, 3, 0)
+        z_last(1, 3, 1)
+        balance(1, 1, 0, allc)
+        amounts(1, 2, halves)
+        z_last(1, 3, 2)
+        z_last(1, 3, 3)
+        for c in (2, 3):
+            for u in range(UNITS):
+                balance(0, u, 1, (c,))
+            finish(0, c, 1)
+        balance(1, 2, 0, allc)
+        for c in allc:
+            amounts(1, 3, [slice(128 * c, 128 * c + 128)])
+        for c in allc:
+            balance(1, 3, 0, (c,))
+            finish(1, c, 0)
+            for u in range(UNITS):
+                balance(1, u, 1, (c,))
+            finish(1, c, 1)

@@ -174,10 +174,10 @@ def tile_equilibrium_mass_balance_s3_kernel(
         def prep_g(u):
             gi = work.tile([P, 512, 4], BF16, name="gi", tag="gi", bufs=2, align_bytes=64)
             for i in range(2):
-                ts = slice(2 * i, 2 * i + 2)
+                ms = slice(64 * i, 64 * i + 64)
                 nc.scalar.copy(
-                    gi[:].rearrange("p (t m) j -> p t m j", t=4)[:, ts],
-                    g_sb[u][:].rearrange("p j (m t) -> p t m j", t=4)[:, ts],
+                    gi[:].rearrange("p (t m) j -> p m t j", t=4)[:, ms],
+                    g_sb[u][:].rearrange("p j (m t) -> p m t j", t=4)[:, ms],
                 )
             g_q[u] = keep.tile([P, 512], U32, name="g_q%d" % u, align_bytes=64)
             g_s[u] = keep.tile([P, 512], U8, name="g_s%d" % u, align_bytes=64)
@@ -261,7 +261,8 @@ def tile_equilibrium_mass_balance_s3_kernel(
                 )
             for cols in halves:
                 nc.vector.tensor_copy(
-                    out=nb[h, u][:, cols, :], in_=flat[:, :, cols].rearrange("p t r -> p r t")
+                    out=nb[h, u][:, cols, :].rearrange("p (r i) t -> p r t i", i=4),
+                    in_=flat[:, :, cols].rearrange("p t (r i) -> p r t i", i=4),
                 )
             for cols in halves:
                 nc.vector.quantize_mx(
@@ -280,9 +281,9 @@ def tile_equilibrium_mass_balance_s3_kernel(
                 n_s[h, u] = keep.tile([P, HALF], U8, name="n_s%d%d" % (h, u), align_bytes=64)
             for cols in chunks:
                 nc.vector.tensor_tensor(
-                    out=nb[h, u][:, cols, :],
-                    in0=e_sb[h, u][:, :, cols].rearrange("p t r -> p r t"),
-                    in1=m_sb[:, u, :].unsqueeze(1).to_broadcast([P, cols.stop - cols.start, 4]),
+                    out=nb[h, u][:, cols, :].rearrange("p (r i) t -> p r t i", i=4),
+                    in0=e_sb[h, u][:, :, cols].rearrange("p t (r i) -> p r t i", i=4),
+                    in1=m_sb[:, u, :].unsqueeze(1).unsqueeze(3).to_broadcast([P, (cols.stop - cols.start) // 4, 4, 4]),
                     op=ALU.mult,
                 )
             for cols in chunks:

@@ -22,6 +22,7 @@ HALF = 512
 ROWS = 4
 UNITS = S // 512
 LG = E // 512
+VCOPY = {(2,0),(3,0)}
 SCALED = {(1, 0), (1, 1), (1, 2)}
 
 
@@ -45,6 +46,10 @@ def tile_equilibrium_mass_balance_s3_kernel(
         ident = keep.tile([P, P], F32, name="ident")
         f_sc_raw = keep.tile([P, LG, S], U8, name="f_sc_raw", align_bytes=64)
         nc.vector.memset(f_sc_raw[:].bitcast(I32), 0)
+        srow = keep.tile([P, E], F32, name="srow")
+        nc.vector.memset(srow[:].bitcast(I32), 0)
+        ones = keep.tile([P, P], F32, name="ones")
+        nc.gpsimd.memset(ones[:], 1.0)
         make_identity(nc, ident[:])
         a_sc = keep.tile([P, UNITS, E], U8, name="a_sc", align_bytes=64)
         nc.gpsimd.memset(a_sc[:].bitcast(I32), 0)
@@ -65,13 +70,17 @@ def tile_equilibrium_mass_balance_s3_kernel(
 
         g_sb, f_sb = {}, {}
 
-        def load_g(u):
-            g_sb[u] = work.tile([P, 4, 512], BF16, name="g_sb", tag="g_sb", bufs=3)
-            nc.sync.dma_start(out=g_sb[u][:], in_=g_v[:, :, 512 * u : 512 * (u + 1)])
+        def load_g(u0, n):
+            t = keep.tile([P, 4, 512 * n], BF16, name="g_sb%d" % u0)
+            nc.sync.dma_start(out=t[:], in_=g_v[:, :, 512 * u0 : 512 * (u0 + n)])
+            for i in range(n):
+                g_sb[u0 + i] = t[:, :, 512 * i : 512 * (i + 1)]
 
-        def load_f(u):
-            f_sb[u] = work.tile([P, LG, 1024], U8, name="f_sb", tag="f_sb", bufs=3)
-            nc.sync.dma_start(out=f_sb[u][:], in_=f_v[:, :, 1024 * u : 1024 * (u + 1)])
+        def load_f(u0, n):
+            t = keep.tile([P, LG, 1024 * n], U8, name="f_sb%d" % u0)
+            nc.sync.dma_start(out=t[:], in_=f_v[:, :, 1024 * u0 : 1024 * (u0 + n)])
+            for i in range(n):
+                f_sb[u0 + i] = t[:, :, 1024 * i : 1024 * (i + 1)]
 
         a_sb = keep.tile([P, UNITS, 2 * E], U8, name="a_sb", align_bytes=64)
 
@@ -84,33 +93,35 @@ def tile_equilibrium_mass_balance_s3_kernel(
             for r in range(4):
                 nc.sync.dma_start(out=words[r:P:32], in_=rows[r])
 
-        load_f(0)
+        load_f(0, 1)
+        nc.sync.dma_start(out=srow[0:1, :], in_=lam_scale)
         load_scales(f_sc_raw, f_scales)
-        scale_b = keep.tile([P, E], F32, name="scale_b")
-        nc.sync.dma_start(out=scale_b[:], in_=lam_scale.rearrange("o k -> (o k)").partition_broadcast(P))
         load_lam(0, slice(0, 2))
         load_phi(0)
-        load_g(0)
+        load_g(0, 1)
         load_lam(0, slice(2, 4))
-        load_f(1)
-        load_g(1)
+        load_f(1, 1)
+        load_g(1, 1)
         load_phi(1)
         m_sb = keep.tile([P, UNITS, 4], BF16, name="m_sb")
         nc.sync.dma_start(out=m_sb[:], in_=m.rearrange("(u p t) -> p u t", p=P, t=4))
         m_f = keep.tile([P, UNITS * 4], F32, name="m_f")
         nc.gpsimd.tensor_copy(out=m_f[:], in_=m_sb[:].rearrange("p u t -> p (u t)"))
-        load_f(2)
-        load_g(2)
-        load_f(3)
-        load_g(3)
+        load_f(2, 2)
+        load_g(2, 2)
         load_lam(1, slice(0, 4))
         load_scales(a_sc, a_scales)
-        load_a(slice(0, 2))
-        load_a(slice(2, 4))
+        load_a(slice(0, 4))
         for h in range(2):
             feed_sb[h] = keep.tile([P, ROWS, E], BF16, name="feed_sb%d" % h)
             nc.sync.dma_start(out=feed_sb[h][:], in_=feed_v[h])
 
+        scale_b = keep.tile([P, E], F32, name="scale_b")
+        for i in range(2):
+            cols = slice(512 * i, 512 * (i + 1))
+            sp = psum.tile([P, 512], F32, name="sp", tag="z", bufs=3)
+            nc.tensor.matmul(sp[:], lhsT=ones[:], rhs=srow[:, cols], start=True, stop=True)
+            nc.scalar.copy(scale_b[:, cols], sp[:])
         phi_q, phi_s, lam_q, lam_s = {}, {}, {}, {}
         phi_t, lam_t = {}, {}
 
@@ -174,10 +185,11 @@ def tile_equilibrium_mass_balance_s3_kernel(
         def prep_g(u):
             gi = work.tile([P, 512, 4], BF16, name="gi", tag="gi", bufs=2, align_bytes=64)
             for i in range(2):
+                copy = nc.vector.tensor_copy if (u, i) in VCOPY else nc.scalar.copy
                 ms = slice(64 * i, 64 * i + 64)
-                nc.scalar.copy(
+                copy(
                     gi[:].rearrange("p (t m) j -> p m t j", t=4)[:, ms],
-                    g_sb[u][:].rearrange("p j (m t) -> p m t j", t=4)[:, ms],
+                    g_sb[u].rearrange("p j (m t) -> p m t j", t=4)[:, ms],
                 )
             g_q[u] = keep.tile([P, 512], U32, name="g_q%d" % u, align_bytes=64)
             g_s[u] = keep.tile([P, 512], U8, name="g_s%d" % u, align_bytes=64)
@@ -251,7 +263,7 @@ def tile_equilibrium_mass_balance_s3_kernel(
         nb = {}
 
         def amounts_s(h, u):
-            nb[h, u] = work.tile([P, HALF, 4], BF16, name="nb", tag="nb", bufs=3, align_bytes=64)
+            nb[h, u] = work.tile([P, HALF, 4], BF16, name="nb", tag="nb", bufs=2, align_bytes=64)
             n_q[h, u] = keep.tile([P, HALF], U32, name="n_q%d%d" % (h, u), align_bytes=64)
             n_s[h, u] = keep.tile([P, HALF], U8, name="n_s%d%d" % (h, u), align_bytes=64)
             flat = work.tile([P, 4, HALF], BF16, name="flat", tag="flat", bufs=2)
@@ -276,7 +288,7 @@ def tile_equilibrium_mass_balance_s3_kernel(
                 amounts_s(h, u)
                 return
             if chunks[0].start == 0:
-                nb[h, u] = work.tile([P, HALF, 4], BF16, name="nb", tag="nb", bufs=3, align_bytes=64)
+                nb[h, u] = work.tile([P, HALF, 4], BF16, name="nb", tag="nb", bufs=2, align_bytes=64)
                 n_q[h, u] = keep.tile([P, HALF], U32, name="n_q%d%d" % (h, u), align_bytes=64)
                 n_s[h, u] = keep.tile([P, HALF], U8, name="n_s%d%d" % (h, u), align_bytes=64)
             for cols in chunks:
@@ -315,7 +327,7 @@ def tile_equilibrium_mass_balance_s3_kernel(
                 )
 
         def finish(h, c, e):
-            o = work.tile([P, 512], F32, name="o", tag="o", bufs=10)
+            o = work.tile([P, 512], F32, name="o", tag="o", bufs=8)
             nc.vector.tensor_tensor(
                 out=o[:], in0=acc[h, c, e][:], in1=feed_sb[h][:, c, 512 * e : 512 * (e + 1)], op=ALU.subtract
             )
@@ -333,7 +345,7 @@ def tile_equilibrium_mass_balance_s3_kernel(
         prep_g(0)
         prep_phi(1, 0, ("acc", 4))
         prep_phi(1, 1, ("acc", 4))
-        z_first(0, 0)
+        z_unit(0, 0)
         for u in range(1, UNITS):
             prep_f(u)
             prep_g(u)
@@ -361,12 +373,9 @@ def tile_equilibrium_mass_balance_s3_kernel(
             finish(0, c, 1)
         balance(1, 0, 0, allc)
         amounts(1, 1, halves)
-        z_last(1, 3, 0)
-        z_last(1, 3, 1)
+        z_unit(1, 3)
         balance(1, 1, 0, allc)
         amounts(1, 2, halves)
-        z_last(1, 3, 2)
-        z_last(1, 3, 3)
         for c in (2, 3):
             for u in range(UNITS):
                 balance(0, u, 1, (c,))

@@ -22,8 +22,6 @@ HALF = 512
 ROWS = 4
 UNITS = S // 512
 LG = E // 512
-VCOPY = {(2,0),(3,0)}
-SCALED = {(1, 0), (1, 1), (1, 2)}
 
 
 def tile_equilibrium_mass_balance_s3_kernel(
@@ -43,13 +41,9 @@ def tile_equilibrium_mass_balance_s3_kernel(
         f_v = f_words.rearrange("k p b -> p k b")
         a_v = a_words.rearrange("k p b -> p k b")
 
-        ident = keep.tile([P, P], F32, name="ident")
         f_sc_raw = keep.tile([P, LG, S], U8, name="f_sc_raw", align_bytes=64)
         nc.vector.memset(f_sc_raw[:].bitcast(I32), 0)
-        srow = keep.tile([P, E], F32, name="srow")
-        nc.vector.memset(srow[:].bitcast(I32), 0)
-        ones = keep.tile([P, P], F32, name="ones")
-        nc.gpsimd.memset(ones[:], 1.0)
+        ident = keep.tile([P, P], F32, name="ident")
         make_identity(nc, ident[:])
         a_sc = keep.tile([P, UNITS, E], U8, name="a_sc", align_bytes=64)
         nc.gpsimd.memset(a_sc[:].bitcast(I32), 0)
@@ -57,16 +51,17 @@ def tile_equilibrium_mass_balance_s3_kernel(
         nc.vector.memset(warm[:], 0.0)
         nc.scalar.activation(warm[:], warm[:], ACT.Exp)
 
-        lam_sb, phi_sb, feed_sb = {}, {}, {}
+        lam_sb, phi_sb, feed_sb = [], [], []
+        for h in range(2):
+            t8 = keep.tile([P, ROWS, E], U8, name="lam_sb%d" % h)
+            tb = keep.tile([P, ROWS, D], BF16, name="phi_sb%d" % h)
+            tf = keep.tile([P, ROWS, E], BF16, name="feed_sb%d" % h)
+            lam_sb.append(t8)
+            phi_sb.append(tb)
+            feed_sb.append(tf)
 
-        def load_lam(h, cs):
-            if h not in lam_sb:
-                lam_sb[h] = keep.tile([P, ROWS, E], U8, name="lam_sb%d" % h)
-            nc.sync.dma_start(out=lam_sb[h][:, cs, :], in_=lam_v[h][:, cs, :])
-
-        def load_phi(h):
-            phi_sb[h] = keep.tile([P, ROWS, D], BF16, name="phi_sb%d" % h)
-            nc.sync.dma_start(out=phi_sb[h][:], in_=phi_v[h])
+        def load_rows(dst, src, h, cs):
+            nc.sync.dma_start(out=dst[h][:, cs, :], in_=src[h][:, cs, :])
 
         g_sb, f_sb = {}, {}
 
@@ -84,308 +79,353 @@ def tile_equilibrium_mass_balance_s3_kernel(
 
         a_sb = keep.tile([P, UNITS, 2 * E], U8, name="a_sb", align_bytes=64)
 
-        def load_a(us):
-            nc.sync.dma_start(out=a_sb[:, us, :], in_=a_v[:, us, :])
-
         def load_scales(dst, src):
             rows = src.bitcast(I32).rearrange("k (q r) n -> r q k n", r=4)
             words = dst[:].bitcast(I32)
             for r in range(4):
                 nc.sync.dma_start(out=words[r:P:32], in_=rows[r])
 
+        l_sc = keep.tile([P, LG, 4], F32, name="l_sc")
+        m_sb = keep.tile([P, UNITS, 4], BF16, name="m_sb")
+        m_f = keep.tile([P, UNITS * 4], F32, name="m_f")
+
         load_f(0, 1)
-        nc.sync.dma_start(out=srow[0:1, :], in_=lam_scale)
         load_scales(f_sc_raw, f_scales)
-        load_lam(0, slice(0, 2))
-        load_phi(0)
+        load_rows(lam_sb, lam_v, 0, slice(0, 2))
+        nc.sync.dma_start(out=l_sc[:], in_=lam_scale.rearrange("o (k p t) -> p (o k) t", p=P, t=4))
+        load_rows(lam_sb, lam_v, 0, slice(2, 4))
+        load_rows(phi_sb, phi_v, 0, slice(0, 4))
         load_g(0, 1)
-        load_lam(0, slice(2, 4))
         load_f(1, 1)
         load_g(1, 1)
-        load_phi(1)
-        m_sb = keep.tile([P, UNITS, 4], BF16, name="m_sb")
+        load_rows(phi_sb, phi_v, 1, slice(0, 4))
         nc.sync.dma_start(out=m_sb[:], in_=m.rearrange("(u p t) -> p u t", p=P, t=4))
-        m_f = keep.tile([P, UNITS * 4], F32, name="m_f")
         nc.gpsimd.tensor_copy(out=m_f[:], in_=m_sb[:].rearrange("p u t -> p (u t)"))
         load_f(2, 2)
         load_g(2, 2)
-        load_lam(1, slice(0, 4))
+        load_rows(lam_sb, lam_v, 1, slice(0, 4))
         load_scales(a_sc, a_scales)
-        load_a(slice(0, 4))
+        nc.sync.dma_start(out=a_sb[:], in_=a_v)
         for h in range(2):
-            feed_sb[h] = keep.tile([P, ROWS, E], BF16, name="feed_sb%d" % h)
-            nc.sync.dma_start(out=feed_sb[h][:], in_=feed_v[h])
+            load_rows(feed_sb, feed_v, h, slice(0, 4))
 
-        scale_b = keep.tile([P, E], F32, name="scale_b")
-        for i in range(2):
-            cols = slice(512 * i, 512 * (i + 1))
-            sp = psum.tile([P, 512], F32, name="sp", tag="z", bufs=3)
-            nc.tensor.matmul(sp[:], lhsT=ones[:], rhs=srow[:, cols], start=True, stop=True)
-            nc.scalar.copy(scale_b[:, cols], sp[:])
-        phi_q, phi_s, lam_q, lam_s = {}, {}, {}, {}
-        phi_t, lam_t = {}, {}
+        phi_q, phi_s, lam_q, lam_s, phi_t, lam_t, tps, casts = {}, {}, {}, {}, {}, {}, {}, {}
 
-        def prep_phi(h, pair, tag):
-            if pair == 0:
-                phi_t[h] = work.tile([P, HALF, 4], BF16, name="phi_t", tag="phi_t", bufs=1, align_bytes=64)
-                phi_q[h] = keep.tile([P, HALF], U32, name="phi_q%d" % h, align_bytes=64)
-                phi_s[h] = keep.tile([P, HALF], U8, name="phi_s%d" % h, align_bytes=64)
-            tp = psum.tile([P, 512], F32, name="tp", tag=tag[0], bufs=tag[1])
+        def begin(h):
+            phi_t[h] = work.tile([P, HALF, 4], BF16, name="phi_t", tag="phi_t", bufs=2, align_bytes=64)
+            phi_q[h] = keep.tile([P, HALF], U32, name="phi_q%d" % h, align_bytes=64)
+            phi_s[h] = keep.tile([P, HALF], U8, name="phi_s%d" % h, align_bytes=64)
+            lam_t[h] = work.tile([P, LG, HALF, 4], BF16, name="lam_t", tag="lam_t", bufs=1, align_bytes=64)
+            lam_q[h] = keep.tile([P, LG, HALF], U32, name="lam_q%d" % h, align_bytes=64)
+            lam_s[h] = keep.tile([P, LG, HALF], U8, name="lam_s%d" % h, align_bytes=64)
+
+        def phi_turn(h, pair):
+            tps[h, "p", pair] = psum.tile([P, 512], F32, name="tp", tag="acc", bufs=4)
             for i in range(2):
                 words = phi_sb[h][:, 2 * pair + i, :].bitcast(F32)
                 for u in range(2):
                     k = 128 * (2 * i + u)
-                    nc.tensor.transpose(tp[:, k : k + 128], words[:, u::2], ident[:])
+                    nc.tensor.transpose(tps[h, "p", pair][:, k : k + 128], words[:, u::2], ident[:])
+
+        def phi_copy(h, pair):
             dst = phi_t[h][:].rearrange("p r t -> p (r t)").bitcast(F32)
             dst = dst.rearrange("p (c r u) -> p c r u", c=4, u=2)
-            nc.scalar.copy(dst[:, 2 * pair : 2 * pair + 2], tp[:].rearrange("p (c u r) -> p c r u", c=2, u=2))
-            if pair == 0:
-                return
-            cols = slice(0, HALF)
-            nc.vector.quantize_mx(
-                out=phi_q[h][:, cols].bitcast(FP8X4),
-                scales=phi_s[h][:, cols],
-                in_=phi_t[h][:, cols, :].rearrange("p r t -> p (r t)"),
-            )
-
-        def prep_lam(h, c, tag):
-            if c == 0:
-                lam_t[h] = work.tile([P, LG, HALF, 4], BF16, name="lam_t", tag="lam_t", bufs=1, align_bytes=64)
-                lam_q[h] = keep.tile([P, LG, HALF], U32, name="lam_q%d" % h, align_bytes=64)
-                lam_s[h] = keep.tile([P, LG, HALF], U8, name="lam_s%d" % h, align_bytes=64)
-            wide = work.tile([P, E], BF16, name="wide", tag="wide", bufs=3)
-            nc.vector.tensor_tensor(
-                out=wide[:], in0=lam_sb[h][:, c, :].bitcast(FP8), in1=scale_b[:], op=ALU.mult
-            )
-            words = wide[:].bitcast(F32)
-            tp = psum.tile([P, 512], F32, name="tp", tag=tag[0], bufs=tag[1])
-            for gg in range(LG):
-                for u in range(2):
-                    k = 128 * (2 * gg + u)
-                    nc.tensor.transpose(
-                        tp[:, k : k + 128], words[:, 256 * gg + u : 256 * (gg + 1) : 2], ident[:]
-                    )
-            dst = lam_t[h][:].rearrange("p g r t -> p (g r t)").bitcast(F32)
-            dst = dst.rearrange("p (g r u) -> p g r u", g=LG, u=2)
             nc.scalar.copy(
-                dst[:, :, 128 * c : 128 * (c + 1), :], tp[:].rearrange("p (g u r) -> p g r u", g=LG, u=2)
+                dst[:, 2 * pair : 2 * pair + 2], tps[h, "p", pair][:].rearrange("p (c u r) -> p c r u", c=2, u=2)
             )
-            n = 1 if h == 0 else 4
-            if c % n == n - 1:
-                cols = slice(128 * (c + 1 - n), 128 * (c + 1))
-                for gg in range(LG):
-                    nc.vector.quantize_mx(
-                        out=lam_q[h][:, gg, cols].bitcast(FP8X4),
-                        scales=lam_s[h][:, gg, cols],
-                        in_=lam_t[h][:, gg, cols, :].rearrange("p r t -> p (r t)"),
+
+        def phi_quant(h):
+            nc.vector.quantize_mx(
+                out=phi_q[h][:].bitcast(FP8X4), scales=phi_s[h][:], in_=phi_t[h][:].rearrange("p r t -> p (r t)")
+            )
+
+        def lam_cast(h, c):
+            casts[h, c] = work.tile([P, E], BF16, name="cast", tag="cast", bufs=3)
+            nc.scalar.copy(casts[h, c][:], lam_sb[h][:, c, :].bitcast(FP8))
+
+        def lam_turn(h, c):
+            words = casts[h, c][:].bitcast(F32)
+            tps[h, c] = psum.tile([P, 512], F32, name="tp", tag="acc", bufs=4)
+            for k in range(LG):
+                for u in range(2):
+                    b = 128 * (2 * k + u)
+                    nc.tensor.transpose(
+                        tps[h, c][:, b : b + 128], words[:, 256 * k + u : 256 * (k + 1) : 2], ident[:]
                     )
 
-        g_q, g_s, f_p, f_sp = {}, {}, {}, {}
-
-        def prep_g(u):
-            gi = work.tile([P, 512, 4], BF16, name="gi", tag="gi", bufs=2, align_bytes=64)
-            for i in range(2):
-                copy = nc.vector.tensor_copy if (u, i) in VCOPY else nc.scalar.copy
-                ms = slice(64 * i, 64 * i + 64)
-                copy(
-                    gi[:].rearrange("p (t m) j -> p m t j", t=4)[:, ms],
-                    g_sb[u].rearrange("p j (m t) -> p m t j", t=4)[:, ms],
+        def lam_mult(h, c):
+            for k in range(LG):
+                vals = tps[h, c][:, 256 * k : 256 * (k + 1)].bitcast(BF16)
+                nc.vector.tensor_tensor(
+                    out=lam_t[h][:, k, 128 * c : 128 * (c + 1), :].rearrange("p r (u e) -> p r u e", e=2),
+                    in0=vals.rearrange("p (u r e) -> p r u e", u=2, e=2),
+                    in1=l_sc[:, k, :].rearrange("p (u e) -> p u e", e=2).unsqueeze(1).to_broadcast([P, P, 2, 2]),
+                    op=ALU.mult,
                 )
+
+        def lam_quant(h, k):
+            nc.vector.quantize_mx(
+                out=lam_q[h][:, k, :].bitcast(FP8X4),
+                scales=lam_s[h][:, k, :],
+                in_=lam_t[h][:, k].rearrange("p r t -> p (r t)"),
+            )
+
+        g_q, g_s, f_p, f_sp, g_i = {}, {}, {}, {}, {}
+
+        def g_lay(u, i, copy):
+            if u not in g_i:
+                g_i[u] = work.tile([P, 512, 4], BF16, name="gi", tag="gi", bufs=2, align_bytes=64)
+            ms = slice(64 * i, 64 * i + 64)
+            copy(
+                g_i[u][:].rearrange("p (t m) j -> p m t j", t=4)[:, ms],
+                g_sb[u].rearrange("p j (m t) -> p m t j", t=4)[:, ms],
+            )
+
+        def g_quant(u):
             g_q[u] = keep.tile([P, 512], U32, name="g_q%d" % u, align_bytes=64)
             g_s[u] = keep.tile([P, 512], U8, name="g_s%d" % u, align_bytes=64)
             nc.vector.quantize_mx(
-                out=g_q[u][:].bitcast(FP8X4), scales=g_s[u][:], in_=gi[:].rearrange("p s j -> p (s j)")
+                out=g_q[u][:].bitcast(FP8X4), scales=g_s[u][:], in_=g_i[u][:].rearrange("p s j -> p (s j)")
             )
 
-        def prep_f(u):
+        def f_move(u):
             f_p[u] = keep.tile([P, LG, 1024], U8, name="f_p%d" % u, align_bytes=64)
-            f_sp[u] = keep.tile([P, LG, 512], U8, name="f_sp%d" % u, align_bytes=64)
-            nc.vector.tensor_copy(
-                out=f_sp[u][:].rearrange("p k (t m) -> p k t m", t=4),
-                in_=f_sc_raw[:, :, 512 * u : 512 * (u + 1)].rearrange("p k (m t) -> p k t m", t=4),
-            )
             for k in range(LG):
                 nc.vector.tensor_copy(
                     out=f_p[u][:, k, :].rearrange("p (t m b) -> p t m b", t=4, b=2),
                     in_=f_sb[u][:, k, :].rearrange("p (m t b) -> p t m b", t=4, b=2),
                 )
 
-        e_sb, n_q, n_s = {}, {}, {}
-
-        def z_passes(h, u, t, cells, dst):
-            cols = slice(128 * t, 128 * (t + 1))
-            nc.tensor.matmul_mx(
-                out=dst, lhsT=g_q[u][:, cols].bitcast(FP8X4), lhsT_scale=g_s[u][:, cols],
-                rhs=phi_q[h][:, cells].bitcast(FP8X4), rhs_scale=phi_s[h][:, cells], start=True, stop=False,
+        def f_scale(u):
+            f_sp[u] = keep.tile([P, LG, 512], U8, name="f_sp%d" % u, align_bytes=64)
+            nc.vector.tensor_copy(
+                out=f_sp[u][:].rearrange("p k (t m) -> p k t m", t=4),
+                in_=f_sc_raw[:, :, 512 * u : 512 * (u + 1)].rearrange("p k (m t) -> p k t m", t=4),
             )
+
+        e_sb, flat, nb, n_q, n_s = {}, {}, {}, {}, {}
+
+        z_ps = {}
+
+        def z_lam(h, u, t):
+            if t == 0:
+                e_sb[h, u] = work.tile([P, 4, HALF], F32, name="e_sb", tag="e_sb", bufs=5)
+            z_ps[h, u, t] = psum.tile([P, HALF], F32, name="zp", tag="z", bufs=3)
             for k in range(LG):
                 nc.tensor.matmul_mx(
-                    out=dst,
+                    out=z_ps[h, u, t][:],
                     lhsT=f_p[u][:, k, 256 * t : 256 * (t + 1)].bitcast(FP4X4),
-                    lhsT_scale=f_sp[u][:, k, cols],
-                    rhs=lam_q[h][:, k, cells].bitcast(FP8X4),
-                    rhs_scale=lam_s[h][:, k, cells],
-                    start=False, stop=(k == LG - 1),
+                    lhsT_scale=f_sp[u][:, k, 128 * t : 128 * (t + 1)],
+                    rhs=lam_q[h][:, k, :].bitcast(FP8X4),
+                    rhs_scale=lam_s[h][:, k, :],
+                    start=(k == 0), stop=False,
                 )
 
-        def new_e(h, u):
-            e_sb[h, u] = work.tile([P, 4, HALF], F32, name="e_sb", tag="e_sb", bufs=4)
+        def z_phi(h, u, t):
+            cols = slice(128 * t, 128 * (t + 1))
+            nc.tensor.matmul_mx(
+                out=z_ps[h, u, t][:], lhsT=g_q[u][:, cols].bitcast(FP8X4), lhsT_scale=g_s[u][:, cols],
+                rhs=phi_q[h][:].bitcast(FP8X4), rhs_scale=phi_s[h][:], start=False, stop=True,
+            )
+            nc.scalar.activation(e_sb[h, u][:, t, :], z_ps[h, u, t][:], ACT.Exp)
 
-        def z_unit(h, u):
-            new_e(h, u)
-            for t in range(4):
-                zp = psum.tile([P, HALF], F32, name="zp", tag="z", bufs=3)
-                z_passes(h, u, t, slice(0, HALF), zp[:])
-                nc.scalar.activation(e_sb[h, u][:, t, :], zp[:], ACT.Exp)
+        def z_exp(h, u, t):
+            z_lam(h, u, t)
+            z_phi(h, u, t)
 
-        def z_first(h, u):
-            new_e(h, u)
-            zps = [
-                psum.tile([P, HALF], F32, name="zp", tag=tag, bufs=n)
-                for tag, n in (("z", 3), ("z", 3), ("z", 3), ("x", 1))
-            ]
-            for c in range(4):
-                for t in range(4):
-                    cells = slice(128 * c, 128 * (c + 1))
-                    z_passes(h, u, t, cells, zps[t][:, cells])
-            for t in range(4):
-                nc.scalar.activation(e_sb[h, u][:, t, :], zps[t][:], ACT.Exp)
-
-        def z_last(h, u, c):
-            if c == 0:
-                new_e(h, u)
-            zp = psum.tile([P, HALF], F32, name="zp", tag="z", bufs=3)
-            cells = slice(128 * c, 128 * (c + 1))
-            for t in range(4):
-                z_passes(h, u, t, cells, zp[:, 128 * t : 128 * (t + 1)])
-            nc.scalar.activation(e_sb[h, u][:, :, cells], zp[:].rearrange("p (t r) -> p t r", t=4), ACT.Exp)
-
-        nb = {}
-
-        def amounts_s(h, u):
+        def n_begin(h, u):
             nb[h, u] = work.tile([P, HALF, 4], BF16, name="nb", tag="nb", bufs=2, align_bytes=64)
             n_q[h, u] = keep.tile([P, HALF], U32, name="n_q%d%d" % (h, u), align_bytes=64)
             n_s[h, u] = keep.tile([P, HALF], U8, name="n_s%d%d" % (h, u), align_bytes=64)
-            flat = work.tile([P, 4, HALF], BF16, name="flat", tag="flat", bufs=2)
-            for t in range(4):
-                nc.scalar.activation(
-                    flat[:, t, :], e_sb[h, u][:, t, :], ACT.Copy, scale=m_f[:, 4 * u + t : 4 * u + t + 1]
-                )
-            for cols in halves:
-                nc.vector.tensor_copy(
-                    out=nb[h, u][:, cols, :].rearrange("p (r i) t -> p r t i", i=4),
-                    in_=flat[:, :, cols].rearrange("p t (r i) -> p r t i", i=4),
-                )
-            for cols in halves:
-                nc.vector.quantize_mx(
-                    out=n_q[h, u][:, cols].bitcast(FP8X4),
-                    scales=n_s[h, u][:, cols],
-                    in_=nb[h, u][:, cols, :].rearrange("p r t -> p (r t)"),
-                )
 
-        def amounts(h, u, chunks):
-            if (h, u) in SCALED:
-                amounts_s(h, u)
-                return
-            if chunks[0].start == 0:
-                nb[h, u] = work.tile([P, HALF, 4], BF16, name="nb", tag="nb", bufs=2, align_bytes=64)
-                n_q[h, u] = keep.tile([P, HALF], U32, name="n_q%d%d" % (h, u), align_bytes=64)
-                n_s[h, u] = keep.tile([P, HALF], U8, name="n_s%d%d" % (h, u), align_bytes=64)
-            for cols in chunks:
-                nc.vector.tensor_tensor(
-                    out=nb[h, u][:, cols, :].rearrange("p (r i) t -> p r t i", i=4),
-                    in0=e_sb[h, u][:, :, cols].rearrange("p t (r i) -> p r t i", i=4),
-                    in1=m_sb[:, u, :].unsqueeze(1).unsqueeze(3).to_broadcast([P, (cols.stop - cols.start) // 4, 4, 4]),
-                    op=ALU.mult,
-                )
-            for cols in chunks:
-                nc.vector.quantize_mx(
-                    out=n_q[h, u][:, cols].bitcast(FP8X4),
-                    scales=n_s[h, u][:, cols],
-                    in_=nb[h, u][:, cols, :].rearrange("p r t -> p (r t)"),
-                )
+        def n_scale(h, u, t):
+            if t == 0:
+                flat[h, u] = work.tile([P, 4, HALF], BF16, name="flat", tag="flat", bufs=2)
+            nc.scalar.activation(
+                flat[h, u][:, t, :], e_sb[h, u][:, t, :], ACT.Copy, scale=m_f[:, 4 * u + t : 4 * u + t + 1]
+            )
+
+        def n_lay(h, u, cols):
+            nc.vector.tensor_copy(
+                out=nb[h, u][:, cols, :].rearrange("p (r i) t -> p r t i", i=4),
+                in_=flat[h, u][:, :, cols].rearrange("p t (r i) -> p r t i", i=4),
+            )
+
+        def n_mult(h, u, cols):
+            nc.vector.tensor_tensor(
+                out=nb[h, u][:, cols, :].rearrange("p (r i) t -> p r t i", i=4),
+                in0=e_sb[h, u][:, :, cols].rearrange("p t (r i) -> p r t i", i=4),
+                in1=m_sb[:, u, :].unsqueeze(1).unsqueeze(3).to_broadcast([P, (cols.stop - cols.start) // 4, 4, 4]),
+                op=ALU.mult,
+            )
+
+        def n_quant(h, u, cols):
+            nc.vector.quantize_mx(
+                out=n_q[h, u][:, cols].bitcast(FP8X4),
+                scales=n_s[h, u][:, cols],
+                in_=nb[h, u][:, cols, :].rearrange("p r t -> p (r t)"),
+            )
 
         acc = {}
 
-        def balance(h, u, e, cs):
-            for c in cs:
-                if (h, c, e) not in acc:
-                    if e == 0:
-                        tag = ("acc", 4)
-                    elif h == 0:
-                        tag = ("x", 1)
-                    else:
-                        tag = (("x", 1), ("z", 3), ("z", 3), ("z", 3))[c]
-                    acc[h, c, e] = psum.tile([P, 512], F32, name="ac", tag=tag[0], bufs=tag[1])
-                cols = slice(128 * c, 128 * (c + 1))
-                nc.tensor.matmul_mx(
-                    out=acc[h, c, e][:],
-                    lhsT=n_q[h, u][:, cols].bitcast(FP8X4), lhsT_scale=n_s[h, u][:, cols],
-                    rhs=a_sb[:, u, 1024 * e : 1024 * (e + 1)].bitcast(FP4X4),
-                    rhs_scale=a_sc[:, u, 512 * e : 512 * (e + 1)],
-                    start=(u == 0), stop=(u == UNITS - 1),
-                )
+        def balance(h, u, e, c):
+            if u == 0:
+                tag = ("acc", 4) if e == 0 else ("x", 1) if c == 0 else ("z", 3)
+                acc[h, c, e] = psum.tile([P, 512], F32, name="ac", tag=tag[0], bufs=tag[1])
+            cols = slice(128 * c, 128 * (c + 1))
+            nc.tensor.matmul_mx(
+                out=acc[h, c, e][:],
+                lhsT=n_q[h, u][:, cols].bitcast(FP8X4), lhsT_scale=n_s[h, u][:, cols],
+                rhs=a_sb[:, u, 1024 * e : 1024 * (e + 1)].bitcast(FP4X4),
+                rhs_scale=a_sc[:, u, 512 * e : 512 * (e + 1)],
+                start=(u == 0), stop=(u == UNITS - 1),
+            )
 
-        def finish(h, c, e):
+        def finish(h, e, c):
             o = work.tile([P, 512], F32, name="o", tag="o", bufs=8)
             nc.vector.tensor_tensor(
                 out=o[:], in0=acc[h, c, e][:], in1=feed_sb[h][:, c, 512 * e : 512 * (e + 1)], op=ALU.subtract
             )
             nc.sync.dma_start(out=out_v[h][:, c, 512 * e : 512 * (e + 1)], in_=o[:])
 
-        allc = range(4)
+        ROW4 = range(4)
         halves = [slice(0, 256), slice(256, 512)]
-        prep_f(0)
-        prep_lam(0, 0, ("acc", 4))
-        prep_lam(0, 1, ("acc", 4))
-        prep_phi(0, 0, ("acc", 4))
-        prep_phi(0, 1, ("acc", 4))
-        prep_lam(0, 2, ("acc", 4))
-        prep_lam(0, 3, ("acc", 4))
-        prep_g(0)
-        prep_phi(1, 0, ("acc", 4))
-        prep_phi(1, 1, ("acc", 4))
-        z_unit(0, 0)
-        for u in range(1, UNITS):
-            prep_f(u)
-            prep_g(u)
-            z_unit(0, u)
-        for i in range(2):
-            prep_lam(1, 2 * i, ("acc", 4))
-            prep_lam(1, 2 * i + 1, ("acc", 4))
-        amounts(0, 0, halves)
-        z_unit(1, 0)
-        amounts(0, 1, halves)
-        balance(0, 0, 0, allc)
-        amounts(0, 2, halves)
-        balance(0, 1, 0, allc)
-        z_unit(1, 1)
-        amounts(0, 3, halves)
-        balance(0, 2, 0, allc)
-        amounts(1, 0, halves)
-        balance(0, 3, 0, allc)
-        for c in allc:
-            finish(0, c, 0)
-        z_unit(1, 2)
-        for c in (0, 1):
-            for u in range(UNITS):
-                balance(0, u, 1, (c,))
-            finish(0, c, 1)
-        balance(1, 0, 0, allc)
-        amounts(1, 1, halves)
-        z_unit(1, 3)
-        balance(1, 1, 0, allc)
-        amounts(1, 2, halves)
-        for c in (2, 3):
-            for u in range(UNITS):
-                balance(0, u, 1, (c,))
-            finish(0, c, 1)
-        balance(1, 2, 0, allc)
-        for c in allc:
-            amounts(1, 3, [slice(128 * c, 128 * c + 128)])
-        for c in allc:
-            balance(1, 3, 0, (c,))
-            finish(1, c, 0)
-            for u in range(UNITS):
-                balance(1, u, 1, (c,))
-            finish(1, c, 1)
+        quarters = [slice(128 * c, 128 * c + 128) for c in ROW4]
+        vc, sc = nc.vector.tensor_copy, nc.scalar.copy
+
+        def n_vector(h, u):
+            n_begin(h, u)
+            for cols in halves:
+                n_mult(h, u, cols)
+            for cols in halves:
+                n_quant(h, u, cols)
+
+        def n_layq(h, u):
+            n_begin(h, u)
+            for cols in halves:
+                n_lay(h, u, cols)
+            for cols in halves:
+                n_quant(h, u, cols)
+
+        with tc.manual_schedule():
+            begin(0)
+            lam_cast(0, 0)
+            f_move(0)
+            lam_cast(0, 1)
+            lam_turn(0, 0)
+            lam_turn(0, 1)
+            f_scale(0)
+            f_scale(1)
+            lam_mult(0, 0)
+            lam_cast(0, 2)
+            lam_mult(0, 1)
+            phi_turn(0, 0)
+            phi_turn(0, 1)
+            lam_turn(0, 2)
+            lam_cast(0, 3)
+            lam_mult(0, 2)
+            lam_turn(0, 3)
+            phi_copy(0, 0)
+            phi_copy(0, 1)
+            g_lay(0, 0, sc)
+            g_lay(0, 1, sc)
+            lam_mult(0, 3)
+            for k in range(LG):
+                lam_quant(0, k)
+            phi_quant(0)
+            g_quant(0)
+            begin(1)
+            for pair in range(2):
+                phi_turn(1, pair)
+            g_lay(1, 0, sc)
+            g_lay(1, 1, vc)
+            f_move(1)
+            for t in range(3):
+                z_lam(0, 0, t)
+            for t in range(3):
+                z_phi(0, 0, t)
+            z_exp(0, 0, 3)
+            for pair in range(2):
+                phi_copy(1, pair)
+            g_quant(1)
+            g_lay(2, 0, vc)
+            g_lay(2, 1, vc)
+            f_move(2)
+            f_scale(2)
+            g_quant(2)
+            phi_quant(1)
+            for t in ROW4:
+                z_exp(0, 1, t)
+            lam_cast(1, 0)
+            g_lay(3, 0, vc)
+            g_lay(3, 1, vc)
+            f_move(3)
+            f_scale(3)
+            g_quant(3)
+            for t in (0, 1):
+                z_exp(0, 2, t)
+            lam_turn(1, 0)
+            lam_cast(1, 1)
+            lam_mult(1, 0)
+            for t in (2, 3):
+                z_exp(0, 2, t)
+            lam_turn(1, 1)
+            lam_cast(1, 2)
+            lam_mult(1, 1)
+            for t in (0, 1):
+                z_exp(0, 3, t)
+            lam_turn(1, 2)
+            lam_cast(1, 3)
+            lam_mult(1, 2)
+            for t in (2, 3):
+                z_exp(0, 3, t)
+            lam_turn(1, 3)
+            lam_mult(1, 3)
+            for k in range(LG):
+                lam_quant(1, k)
+            n_vector(0, 0)
+            for t in ROW4:
+                z_exp(1, 0, t)
+            n_vector(0, 1)
+            for c in ROW4:
+                balance(0, 0, 0, c)
+            n_vector(0, 2)
+            for t in ROW4:
+                z_exp(1, 1, t)
+            for t in ROW4:
+                n_scale(1, 0, t)
+            for u in (1, 2):
+                for c in ROW4:
+                    balance(0, u, 0, c)
+            n_vector(0, 3)
+            for t in ROW4:
+                z_exp(1, 2, t)
+            n_layq(1, 0)
+            for t in ROW4:
+                n_scale(1, 1, t)
+            for c in ROW4:
+                balance(0, 3, 0, c)
+                finish(0, 0, c)
+            for t in ROW4:
+                z_exp(1, 3, t)
+            n_layq(1, 1)
+            for c in ROW4:
+                for u in range(UNITS):
+                    balance(0, u, 1, c)
+            n_vector(1, 2)
+            n_begin(1, 3)
+            for cols in quarters:
+                n_mult(1, 3, cols)
+            for c in ROW4:
+                finish(0, 1, c)
+            for cols in quarters:
+                n_quant(1, 3, cols)
+            for u in range(3):
+                for c in ROW4:
+                    balance(1, u, 0, c)
+            for c in ROW4:
+                balance(1, 3, 0, c)
+                finish(1, 0, c)
+                for u in range(UNITS):
+                    balance(1, u, 1, c)
+                finish(1, 1, c)

@@ -89,9 +89,9 @@ def tile_equilibrium_mass_balance_s3_kernel(
         m_sb = keep.tile([P, UNITS, 4], BF16, name="m_sb")
         m_f = keep.tile([P, UNITS * 4], F32, name="m_f")
 
+        load_rows(lam_sb, lam_v, 0, slice(0, 2))
         load_f(0, 1)
         load_scales(f_sc_raw, f_scales)
-        load_rows(lam_sb, lam_v, 0, slice(0, 2))
         nc.sync.dma_start(out=l_sc[:], in_=lam_scale.rearrange("o (k p t) -> p (o k) t", p=P, t=4))
         load_rows(lam_sb, lam_v, 0, slice(2, 4))
         load_rows(phi_sb, phi_v, 0, slice(0, 4))
@@ -207,19 +207,17 @@ def tile_equilibrium_mass_balance_s3_kernel(
 
         z_ps = {}
 
-        def z_lam(h, u, t):
-            if t == 0:
-                e_sb[h, u] = work.tile([P, 4, HALF], F32, name="e_sb", tag="e_sb", bufs=5)
-            z_ps[h, u, t] = psum.tile([P, HALF], F32, name="zp", tag="z", bufs=3)
-            for k in range(LG):
-                nc.tensor.matmul_mx(
-                    out=z_ps[h, u, t][:],
-                    lhsT=f_p[u][:, k, 256 * t : 256 * (t + 1)].bitcast(FP4X4),
-                    lhsT_scale=f_sp[u][:, k, 128 * t : 128 * (t + 1)],
-                    rhs=lam_q[h][:, k, :].bitcast(FP8X4),
-                    rhs_scale=lam_s[h][:, k, :],
-                    start=(k == 0), stop=False,
-                )
+        def z_lam(h, u, t, k):
+            if k == 0:
+                z_ps[h, u, t] = psum.tile([P, HALF], F32, name="zp", tag="z", bufs=4)
+            nc.tensor.matmul_mx(
+                out=z_ps[h, u, t][:],
+                lhsT=f_p[u][:, k, 256 * t : 256 * (t + 1)].bitcast(FP4X4),
+                lhsT_scale=f_sp[u][:, k, 128 * t : 128 * (t + 1)],
+                rhs=lam_q[h][:, k, :].bitcast(FP8X4),
+                rhs_scale=lam_s[h][:, k, :],
+                start=(k == 0), stop=False,
+            )
 
         def z_phi(h, u, t):
             cols = slice(128 * t, 128 * (t + 1))
@@ -227,11 +225,17 @@ def tile_equilibrium_mass_balance_s3_kernel(
                 out=z_ps[h, u, t][:], lhsT=g_q[u][:, cols].bitcast(FP8X4), lhsT_scale=g_s[u][:, cols],
                 rhs=phi_q[h][:].bitcast(FP8X4), rhs_scale=phi_s[h][:], start=False, stop=True,
             )
+
+        def exp(h, u, t):
+            if t == 0:
+                e_sb[h, u] = work.tile([P, 4, HALF], F32, name="e_sb", tag="e_sb", bufs=5)
             nc.scalar.activation(e_sb[h, u][:, t, :], z_ps[h, u, t][:], ACT.Exp)
 
         def z_exp(h, u, t):
-            z_lam(h, u, t)
+            for k in range(LG):
+                z_lam(h, u, t, k)
             z_phi(h, u, t)
+            exp(h, u, t)
 
         def n_begin(h, u):
             nb[h, u] = work.tile([P, HALF, 4], BF16, name="nb", tag="nb", bufs=2, align_bytes=64)
@@ -270,7 +274,7 @@ def tile_equilibrium_mass_balance_s3_kernel(
 
         def balance(h, u, e, c):
             if u == 0:
-                tag = ("acc", 4) if e == 0 else ("x", 1) if c == 0 else ("z", 3)
+                tag = ("acc", 4) if e == 0 else ("z", 4)
                 acc[h, c, e] = psum.tile([P, 512], F32, name="ac", tag=tag[0], bufs=tag[1])
             cols = slice(128 * c, 128 * (c + 1))
             nc.tensor.matmul_mx(
@@ -281,12 +285,22 @@ def tile_equilibrium_mass_balance_s3_kernel(
                 start=(u == 0), stop=(u == UNITS - 1),
             )
 
-        def finish(h, e, c):
-            o = work.tile([P, 512], F32, name="o", tag="o", bufs=8)
-            nc.vector.tensor_tensor(
-                out=o[:], in0=acc[h, c, e][:], in1=feed_sb[h][:, c, 512 * e : 512 * (e + 1)], op=ALU.subtract
-            )
-            nc.sync.dma_start(out=out_v[h][:, c, 512 * e : 512 * (e + 1)], in_=o[:])
+        def finish(h, e, c, parts=1):
+            w = 512 // parts
+            for i in range(parts):
+                cols = slice(512 * e + w * i, 512 * e + w * (i + 1))
+                o = work.tile([P, w], F32, name="o", tag="o", bufs=8)
+                nc.vector.tensor_tensor(
+                    out=o[:], in0=acc[h, c, e][:, w * i : w * (i + 1)], in1=feed_sb[h][:, c, cols], op=ALU.subtract
+                )
+                nc.sync.dma_start(out=out_v[h][:, c, cols], in_=o[:])
+
+        def warm_up(n):
+            wp = psum.tile([P, 512], F32, name="wp", tag="acc", bufs=4)
+            for i in range(n):
+                nc.tensor.matmul(
+                    wp[:], lhsT=phi_sb[0][:, 0, 0:P], rhs=phi_sb[0][:, 0, :], start=True, stop=True
+                )
 
         ROW4 = range(4)
         halves = [slice(0, 256), slice(256, 512)]
@@ -307,22 +321,39 @@ def tile_equilibrium_mass_balance_s3_kernel(
             for cols in halves:
                 n_quant(h, u, cols)
 
+        def z4(h, u, ts=ROW4):
+            for t in ts:
+                z_exp(h, u, t)
+
+        def scale4(h, u):
+            for t in ROW4:
+                n_scale(h, u, t)
+
+        def bal4(h, u, e):
+            for c in ROW4:
+                balance(h, u, e, c)
+
+        def balu(h, e, c):
+            for u in range(UNITS):
+                balance(h, u, e, c)
+
+        begin(0)
+        begin(1)
         with tc.manual_schedule():
-            begin(0)
             lam_cast(0, 0)
             f_move(0)
-            lam_cast(0, 1)
-            lam_turn(0, 0)
-            lam_turn(0, 1)
             f_scale(0)
-            f_scale(1)
-            lam_mult(0, 0)
+            lam_cast(0, 1)
+            for c in (0, 1):
+                lam_turn(0, c)
             lam_cast(0, 2)
-            lam_mult(0, 1)
             phi_turn(0, 0)
             phi_turn(0, 1)
+            f_scale(1)
+            lam_mult(0, 0)
             lam_turn(0, 2)
             lam_cast(0, 3)
+            lam_mult(0, 1)
             lam_mult(0, 2)
             lam_turn(0, 3)
             phi_copy(0, 0)
@@ -330,102 +361,79 @@ def tile_equilibrium_mass_balance_s3_kernel(
             g_lay(0, 0, sc)
             g_lay(0, 1, sc)
             lam_mult(0, 3)
+            lam_quant(0, 0)
+            warm_up(6)
+            lam_quant(0, 1)
             for k in range(LG):
-                lam_quant(0, k)
+                for t in ROW4:
+                    z_lam(0, 0, t, k)
             phi_quant(0)
             g_quant(0)
-            begin(1)
-            for pair in range(2):
-                phi_turn(1, pair)
             g_lay(1, 0, sc)
             g_lay(1, 1, vc)
             f_move(1)
-            for t in range(3):
-                z_lam(0, 0, t)
-            for t in range(3):
-                z_phi(0, 0, t)
-            z_exp(0, 0, 3)
-            for pair in range(2):
-                phi_copy(1, pair)
             g_quant(1)
+            for t in ROW4:
+                z_phi(0, 0, t)
+                exp(0, 0, t)
+            phi_turn(1, 0)
+            phi_turn(1, 1)
+            phi_copy(1, 0)
+            phi_copy(1, 1)
+            lam_cast(1, 0)
             g_lay(2, 0, vc)
             g_lay(2, 1, vc)
             f_move(2)
             f_scale(2)
             g_quant(2)
-            phi_quant(1)
-            for t in ROW4:
-                z_exp(0, 1, t)
-            lam_cast(1, 0)
+            z4(0, 1)
+            lam_cast(1, 1)
             g_lay(3, 0, vc)
             g_lay(3, 1, vc)
             f_move(3)
             f_scale(3)
             g_quant(3)
-            for t in (0, 1):
-                z_exp(0, 2, t)
+            z4(0, 2, (0, 1))
             lam_turn(1, 0)
-            lam_cast(1, 1)
             lam_mult(1, 0)
-            for t in (2, 3):
-                z_exp(0, 2, t)
-            lam_turn(1, 1)
             lam_cast(1, 2)
+            z4(0, 2, (2, 3))
+            lam_turn(1, 1)
             lam_mult(1, 1)
-            for t in (0, 1):
-                z_exp(0, 3, t)
             lam_turn(1, 2)
-            lam_cast(1, 3)
             lam_mult(1, 2)
-            for t in (2, 3):
-                z_exp(0, 3, t)
+            lam_cast(1, 3)
+            z4(0, 3, (0, 1))
             lam_turn(1, 3)
             lam_mult(1, 3)
             for k in range(LG):
                 lam_quant(1, k)
+            phi_quant(1)
+            z4(0, 3, (2, 3))
             n_vector(0, 0)
-            for t in ROW4:
-                z_exp(1, 0, t)
-            n_vector(0, 1)
-            for c in ROW4:
-                balance(0, 0, 0, c)
+            scale4(0, 1)
+            z4(1, 0)
+            n_layq(0, 1)
+            z4(1, 1)
+            scale4(1, 0)
             n_vector(0, 2)
-            for t in ROW4:
-                z_exp(1, 1, t)
-            for t in ROW4:
-                n_scale(1, 0, t)
-            for u in (1, 2):
-                for c in ROW4:
-                    balance(0, u, 0, c)
+            z4(1, 2)
+            scale4(1, 1)
             n_vector(0, 3)
-            for t in ROW4:
-                z_exp(1, 2, t)
+            z4(1, 3)
             n_layq(1, 0)
-            for t in ROW4:
-                n_scale(1, 1, t)
-            for c in ROW4:
-                balance(0, 3, 0, c)
-                finish(0, 0, c)
-            for t in ROW4:
-                z_exp(1, 3, t)
             n_layq(1, 1)
             for c in ROW4:
-                for u in range(UNITS):
-                    balance(0, u, 1, c)
+                for e in range(2):
+                    balu(0, e, c)
+            finish(0, 0, 0)
             n_vector(1, 2)
-            n_begin(1, 3)
-            for cols in quarters:
-                n_mult(1, 3, cols)
+            n_vector(1, 3)
+            finish(0, 1, 0)
+            for c in (1, 2, 3):
+                for e in range(2):
+                    finish(0, e, c)
             for c in ROW4:
-                finish(0, 1, c)
-            for cols in quarters:
-                n_quant(1, 3, cols)
-            for u in range(3):
-                for c in ROW4:
-                    balance(1, u, 0, c)
-            for c in ROW4:
-                balance(1, 3, 0, c)
-                finish(1, 0, c)
-                for u in range(UNITS):
-                    balance(1, u, 1, c)
-                finish(1, 1, c)
+                for e in range(2):
+                    balu(1, e, c)
+                    finish(1, e, c, 2 if (c, e) == (3, 1) else 1)

from contextlib import ExitStack

import concourse.mybir as mybir
from concourse.masks import make_identity

B, E, D, S = 1024, 1024, 512, 2048
FLOPS = 2 * B * S * (E + D) + 2 * B * S * E

F32 = mybir.dt.float32
BF16 = mybir.dt.bfloat16
U32 = mybir.dt.uint32
I32 = mybir.dt.int32
U8 = mybir.dt.uint8
FP8 = mybir.dt.float8_e4m3fn
FP8X4 = mybir.dt.float8_e4m3fn_x4
FP4X4 = mybir.dt.float4_e2m1fn_x4
ALU = mybir.AluOpType
ACT = mybir.ActivationFunctionType

P = 128
HALF = 512
ROWS = 4
UNITS = S // 512
LG = E // 512


def tile_equilibrium_mass_balance_s3_kernel(
    tc, lam_bytes, lam_scale, f_words, f_scales, phi, g, m, a_words, a_scales, feed, out
):
    nc = tc.nc
    with ExitStack() as ctx:
        keep = ctx.enter_context(tc.tile_pool(name="keep", bufs=1))
        work = ctx.enter_context(tc.tile_pool(name="work", bufs=2))
        psum = ctx.enter_context(tc.psum_pool(name="psum", bufs=1))

        lam_v = lam_bytes.rearrange("(h p c) k -> h p c k", h=2, c=ROWS)
        phi_v = phi.rearrange("(h p c) k -> h p c k", h=2, c=ROWS)
        feed_v = feed.rearrange("(h p c) e -> h p c e", h=2, c=ROWS)
        out_v = out.rearrange("(h p c) e -> h p c e", h=2, c=ROWS)
        g_v = g.rearrange("(p j) s -> p j s", j=4)
        f_v = f_words.rearrange("k p b -> p k b")
        a_v = a_words.rearrange("k p b -> p k b")

        f_sc_raw = keep.tile([P, LG, S], U8, name="f_sc_raw", align_bytes=64)
        nc.vector.memset(f_sc_raw[:].bitcast(I32), 0)
        ident = keep.tile([P, P], F32, name="ident")
        make_identity(nc, ident[:])
        a_sc = keep.tile([P, UNITS, E], U8, name="a_sc", align_bytes=64)
        nc.gpsimd.memset(a_sc[:].bitcast(I32), 0)
        warm = keep.tile([P, 1], F32, name="warm")
        nc.vector.memset(warm[:], 0.0)
        nc.scalar.activation(warm[:], warm[:], ACT.Exp)

        lam_sb, phi_sb, feed_sb = [], [], []
        for h in range(2):
            t8 = keep.tile([P, ROWS, E], U8, name="lam_sb%d" % h)
            tb = keep.tile([P, ROWS, D], BF16, name="phi_sb%d" % h)
            tf = keep.tile([P, ROWS, E], BF16, name="feed_sb%d" % h)
            lam_sb.append(t8)
            phi_sb.append(tb)
            feed_sb.append(tf)

        def load_rows(dst, src, h, cs):
            nc.sync.dma_start(out=dst[h][:, cs, :], in_=src[h][:, cs, :])

        g_sb, f_sb = {}, {}

        def load_g(u0, n):
            t = keep.tile([P, 4, 512 * n], BF16, name="g_sb%d" % u0)
            nc.sync.dma_start(out=t[:], in_=g_v[:, :, 512 * u0 : 512 * (u0 + n)])
            for i in range(n):
                g_sb[u0 + i] = t[:, :, 512 * i : 512 * (i + 1)]

        def load_f(u0, n):
            t = keep.tile([P, LG, 1024 * n], U8, name="f_sb%d" % u0)
            nc.sync.dma_start(out=t[:], in_=f_v[:, :, 1024 * u0 : 1024 * (u0 + n)])
            for i in range(n):
                f_sb[u0 + i] = t[:, :, 1024 * i : 1024 * (i + 1)]

        a_sb = keep.tile([P, UNITS, 2 * E], U8, name="a_sb", align_bytes=64)

        def load_scales(dst, src):
            rows = src.bitcast(I32).rearrange("k (q r) n -> r q k n", r=4)
            words = dst[:].bitcast(I32)
            for r in range(4):
                nc.sync.dma_start(out=words[r:P:32], in_=rows[r])

        l_sc = keep.tile([P, LG, 4], F32, name="l_sc")
        m_sb = keep.tile([P, UNITS, 4], BF16, name="m_sb")
        m_f = keep.tile([P, UNITS * 4], F32, name="m_f")

        load_rows(lam_sb, lam_v, 0, slice(0, 2))
        load_f(0, 1)
        load_scales(f_sc_raw, f_scales)
        nc.sync.dma_start(out=l_sc[:], in_=lam_scale.rearrange("o (k p t) -> p (o k) t", p=P, t=4))
        load_rows(lam_sb, lam_v, 0, slice(2, 4))
        load_rows(phi_sb, phi_v, 0, slice(0, 4))
        load_g(0, 1)
        load_f(1, 1)
        load_g(1, 1)
        load_rows(phi_sb, phi_v, 1, slice(0, 4))
        nc.sync.dma_start(out=m_sb[:], in_=m.rearrange("(u p t) -> p u t", p=P, t=4))
        nc.gpsimd.tensor_copy(out=m_f[:], in_=m_sb[:].rearrange("p u t -> p (u t)"))
        load_f(2, 2)
        load_g(2, 2)
        load_rows(lam_sb, lam_v, 1, slice(0, 4))
        load_scales(a_sc, a_scales)
        nc.sync.dma_start(out=a_sb[:], in_=a_v)
        for h in range(2):
            load_rows(feed_sb, feed_v, h, slice(0, 4))

        phi_q, phi_s, lam_q, lam_s, phi_t, lam_t, tps, casts = {}, {}, {}, {}, {}, {}, {}, {}

        def begin(h):
            phi_t[h] = work.tile([P, HALF, 4], BF16, name="phi_t", tag="phi_t", bufs=2, align_bytes=64)
            phi_q[h] = keep.tile([P, HALF], U32, name="phi_q%d" % h, align_bytes=64)
            phi_s[h] = keep.tile([P, HALF], U8, name="phi_s%d" % h, align_bytes=64)
            lam_t[h] = work.tile([P, LG, HALF, 4], BF16, name="lam_t", tag="lam_t", bufs=1, align_bytes=64)
            lam_q[h] = keep.tile([P, LG, HALF], U32, name="lam_q%d" % h, align_bytes=64)
            lam_s[h] = keep.tile([P, LG, HALF], U8, name="lam_s%d" % h, align_bytes=64)

        def phi_turn(h, pair):
            tps[h, "p", pair] = psum.tile([P, 512], F32, name="tp", tag="acc", bufs=4)
            for i in range(2):
                words = phi_sb[h][:, 2 * pair + i, :].bitcast(F32)
                for u in range(2):
                    k = 128 * (2 * i + u)
                    nc.tensor.transpose(tps[h, "p", pair][:, k : k + 128], words[:, u::2], ident[:])

        def phi_copy(h, pair):
            dst = phi_t[h][:].rearrange("p r t -> p (r t)").bitcast(F32)
            dst = dst.rearrange("p (c r u) -> p c r u", c=4, u=2)
            nc.scalar.copy(
                dst[:, 2 * pair : 2 * pair + 2], tps[h, "p", pair][:].rearrange("p (c u r) -> p c r u", c=2, u=2)
            )

        def phi_quant(h):
            nc.vector.quantize_mx(
                out=phi_q[h][:].bitcast(FP8X4), scales=phi_s[h][:], in_=phi_t[h][:].rearrange("p r t -> p (r t)")
            )

        def lam_cast(h, c):
            casts[h, c] = work.tile([P, E], BF16, name="cast", tag="cast", bufs=3)
            nc.scalar.copy(casts[h, c][:], lam_sb[h][:, c, :].bitcast(FP8))

        def lam_turn(h, c):
            words = casts[h, c][:].bitcast(F32)
            tps[h, c] = psum.tile([P, 512], F32, name="tp", tag="acc", bufs=4)
            for k in range(LG):
                for u in range(2):
                    b = 128 * (2 * k + u)
                    nc.tensor.transpose(
                        tps[h, c][:, b : b + 128], words[:, 256 * k + u : 256 * (k + 1) : 2], ident[:]
                    )

        def lam_mult(h, c):
            for k in range(LG):
                vals = tps[h, c][:, 256 * k : 256 * (k + 1)].bitcast(BF16)
                nc.vector.tensor_tensor(
                    out=lam_t[h][:, k, 128 * c : 128 * (c + 1), :].rearrange("p r (u e) -> p r u e", e=2),
                    in0=vals.rearrange("p (u r e) -> p r u e", u=2, e=2),
                    in1=l_sc[:, k, :].rearrange("p (u e) -> p u e", e=2).unsqueeze(1).to_broadcast([P, P, 2, 2]),
                    op=ALU.mult,
                )

        def lam_quant(h, k):
            nc.vector.quantize_mx(
                out=lam_q[h][:, k, :].bitcast(FP8X4),
                scales=lam_s[h][:, k, :],
                in_=lam_t[h][:, k].rearrange("p r t -> p (r t)"),
            )

        g_q, g_s, f_p, f_sp, g_i = {}, {}, {}, {}, {}

        def g_lay(u, i, copy):
            if u not in g_i:
                g_i[u] = work.tile([P, 512, 4], BF16, name="gi", tag="gi", bufs=2, align_bytes=64)
            ms = slice(64 * i, 64 * i + 64)
            copy(
                g_i[u][:].rearrange("p (t m) j -> p m t j", t=4)[:, ms],
                g_sb[u].rearrange("p j (m t) -> p m t j", t=4)[:, ms],
            )

        def g_quant(u):
            g_q[u] = keep.tile([P, 512], U32, name="g_q%d" % u, align_bytes=64)
            g_s[u] = keep.tile([P, 512], U8, name="g_s%d" % u, align_bytes=64)
            nc.vector.quantize_mx(
                out=g_q[u][:].bitcast(FP8X4), scales=g_s[u][:], in_=g_i[u][:].rearrange("p s j -> p (s j)")
            )

        def f_move(u):
            f_p[u] = keep.tile([P, LG, 1024], U8, name="f_p%d" % u, align_bytes=64)
            for k in range(LG):
                nc.vector.tensor_copy(
                    out=f_p[u][:, k, :].rearrange("p (t m b) -> p t m b", t=4, b=2),
                    in_=f_sb[u][:, k, :].rearrange("p (m t b) -> p t m b", t=4, b=2),
                )

        def f_scale(u):
            f_sp[u] = keep.tile([P, LG, 512], U8, name="f_sp%d" % u, align_bytes=64)
            nc.vector.tensor_copy(
                out=f_sp[u][:].rearrange("p k (t m) -> p k t m", t=4),
                in_=f_sc_raw[:, :, 512 * u : 512 * (u + 1)].rearrange("p k (m t) -> p k t m", t=4),
            )

        e_sb, flat, nb, n_q, n_s = {}, {}, {}, {}, {}

        z_ps = {}

        def z_lam(h, u, t, k):
            if k == 0:
                z_ps[h, u, t] = psum.tile([P, HALF], F32, name="zp", tag="z", bufs=4)
            nc.tensor.matmul_mx(
                out=z_ps[h, u, t][:],
                lhsT=f_p[u][:, k, 256 * t : 256 * (t + 1)].bitcast(FP4X4),
                lhsT_scale=f_sp[u][:, k, 128 * t : 128 * (t + 1)],
                rhs=lam_q[h][:, k, :].bitcast(FP8X4),
                rhs_scale=lam_s[h][:, k, :],
                start=(k == 0), stop=False,
            )

        def z_phi(h, u, t):
            cols = slice(128 * t, 128 * (t + 1))
            nc.tensor.matmul_mx(
                out=z_ps[h, u, t][:], lhsT=g_q[u][:, cols].bitcast(FP8X4), lhsT_scale=g_s[u][:, cols],
                rhs=phi_q[h][:].bitcast(FP8X4), rhs_scale=phi_s[h][:], start=False, stop=True,
            )

        def exp(h, u, t):
            if t == 0:
                e_sb[h, u] = work.tile([P, 4, HALF], F32, name="e_sb", tag="e_sb", bufs=5)
            nc.scalar.activation(e_sb[h, u][:, t, :], z_ps[h, u, t][:], ACT.Exp)

        def z_exp(h, u, t):
            for k in range(LG):
                z_lam(h, u, t, k)
            z_phi(h, u, t)
            exp(h, u, t)

        def n_begin(h, u):
            nb[h, u] = work.tile([P, HALF, 4], BF16, name="nb", tag="nb", bufs=2, align_bytes=64)
            n_q[h, u] = keep.tile([P, HALF], U32, name="n_q%d%d" % (h, u), align_bytes=64)
            n_s[h, u] = keep.tile([P, HALF], U8, name="n_s%d%d" % (h, u), align_bytes=64)

        def n_scale(h, u, t):
            if t == 0:
                flat[h, u] = work.tile([P, 4, HALF], BF16, name="flat", tag="flat", bufs=2)
            nc.scalar.activation(
                flat[h, u][:, t, :], e_sb[h, u][:, t, :], ACT.Copy, scale=m_f[:, 4 * u + t : 4 * u + t + 1]
            )

        def n_lay(h, u, cols):
            nc.vector.tensor_copy(
                out=nb[h, u][:, cols, :].rearrange("p (r i) t -> p r t i", i=4),
                in_=flat[h, u][:, :, cols].rearrange("p t (r i) -> p r t i", i=4),
            )

        def n_mult(h, u, cols):
            nc.vector.tensor_tensor(
                out=nb[h, u][:, cols, :].rearrange("p (r i) t -> p r t i", i=4),
                in0=e_sb[h, u][:, :, cols].rearrange("p t (r i) -> p r t i", i=4),
                in1=m_sb[:, u, :].unsqueeze(1).unsqueeze(3).to_broadcast([P, (cols.stop - cols.start) // 4, 4, 4]),
                op=ALU.mult,
            )

        def n_quant(h, u, cols):
            nc.vector.quantize_mx(
                out=n_q[h, u][:, cols].bitcast(FP8X4),
                scales=n_s[h, u][:, cols],
                in_=nb[h, u][:, cols, :].rearrange("p r t -> p (r t)"),
            )

        acc = {}

        def balance(h, u, e, c):
            if u == 0:
                tag = ("acc", 4) if e == 0 else ("z", 4)
                acc[h, c, e] = psum.tile([P, 512], F32, name="ac", tag=tag[0], bufs=tag[1])
            cols = slice(128 * c, 128 * (c + 1))
            nc.tensor.matmul_mx(
                out=acc[h, c, e][:],
                lhsT=n_q[h, u][:, cols].bitcast(FP8X4), lhsT_scale=n_s[h, u][:, cols],
                rhs=a_sb[:, u, 1024 * e : 1024 * (e + 1)].bitcast(FP4X4),
                rhs_scale=a_sc[:, u, 512 * e : 512 * (e + 1)],
                start=(u == 0), stop=(u == UNITS - 1),
            )

        def finish(h, e, c, parts=1):
            w = 512 // parts
            for i in range(parts):
                cols = slice(512 * e + w * i, 512 * e + w * (i + 1))
                o = work.tile([P, w], F32, name="o", tag="o", bufs=8)
                nc.vector.tensor_tensor(
                    out=o[:], in0=acc[h, c, e][:, w * i : w * (i + 1)], in1=feed_sb[h][:, c, cols], op=ALU.subtract
                )
                nc.sync.dma_start(out=out_v[h][:, c, cols], in_=o[:])

        def warm_up(n):
            wp = psum.tile([P, 512], F32, name="wp", tag="acc", bufs=4)
            for i in range(n):
                nc.tensor.matmul(
                    wp[:], lhsT=phi_sb[0][:, 0, 0:P], rhs=phi_sb[0][:, 0, :], start=True, stop=True
                )

        ROW4 = range(4)
        halves = [slice(0, 256), slice(256, 512)]
        quarters = [slice(128 * c, 128 * c + 128) for c in ROW4]
        vc, sc = nc.vector.tensor_copy, nc.scalar.copy

        def n_vector(h, u):
            n_begin(h, u)
            for cols in halves:
                n_mult(h, u, cols)
            for cols in halves:
                n_quant(h, u, cols)

        def n_layq(h, u):
            n_begin(h, u)
            for cols in halves:
                n_lay(h, u, cols)
            for cols in halves:
                n_quant(h, u, cols)

        def z4(h, u, ts=ROW4):
            for t in ts:
                z_exp(h, u, t)

        def scale4(h, u):
            for t in ROW4:
                n_scale(h, u, t)

        def bal4(h, u, e):
            for c in ROW4:
                balance(h, u, e, c)

        def balu(h, e, c):
            for u in range(UNITS):
                balance(h, u, e, c)

        begin(0)
        begin(1)
        with tc.manual_schedule():
            lam_cast(0, 0)
            f_move(0)
            f_scale(0)
            lam_cast(0, 1)
            for c in (0, 1):
                lam_turn(0, c)
            lam_cast(0, 2)
            phi_turn(0, 0)
            phi_turn(0, 1)
            f_scale(1)
            lam_mult(0, 0)
            lam_turn(0, 2)
            lam_cast(0, 3)
            lam_mult(0, 1)
            lam_mult(0, 2)
            lam_turn(0, 3)
            phi_copy(0, 0)
            phi_copy(0, 1)
            g_lay(0, 0, sc)
            g_lay(0, 1, sc)
            lam_mult(0, 3)
            lam_quant(0, 0)
            warm_up(6)
            lam_quant(0, 1)
            for k in range(LG):
                for t in ROW4:
                    z_lam(0, 0, t, k)
            phi_quant(0)
            g_quant(0)
            g_lay(1, 0, sc)
            g_lay(1, 1, vc)
            f_move(1)
            g_quant(1)
            for t in ROW4:
                z_phi(0, 0, t)
                exp(0, 0, t)
            phi_turn(1, 0)
            phi_turn(1, 1)
            phi_copy(1, 0)
            phi_copy(1, 1)
            lam_cast(1, 0)
            g_lay(2, 0, vc)
            g_lay(2, 1, vc)
            f_move(2)
            f_scale(2)
            g_quant(2)
            z4(0, 1)
            lam_cast(1, 1)
            g_lay(3, 0, vc)
            g_lay(3, 1, vc)
            f_move(3)
            f_scale(3)
            g_quant(3)
            z4(0, 2, (0, 1))
            lam_turn(1, 0)
            lam_mult(1, 0)
            lam_cast(1, 2)
            z4(0, 2, (2, 3))
            lam_turn(1, 1)
            lam_mult(1, 1)
            lam_turn(1, 2)
            lam_mult(1, 2)
            lam_cast(1, 3)
            z4(0, 3, (0, 1))
            lam_turn(1, 3)
            lam_mult(1, 3)
            for k in range(LG):
                lam_quant(1, k)
            phi_quant(1)
            z4(0, 3, (2, 3))
            n_vector(0, 0)
            scale4(0, 1)
            z4(1, 0)
            n_layq(0, 1)
            z4(1, 1)
            scale4(1, 0)
            n_vector(0, 2)
            z4(1, 2)
            scale4(1, 1)
            n_vector(0, 3)
            z4(1, 3)
            n_layq(1, 0)
            n_layq(1, 1)
            for c in ROW4:
                for e in range(2):
                    balu(0, e, c)
            finish(0, 0, 0)
            n_vector(1, 2)
            n_vector(1, 3)
            finish(0, 1, 0)
            for c in (1, 2, 3):
                for e in range(2):
                    finish(0, e, c)
            for c in ROW4:
                for e in range(2):
                    balu(1, e, c)
                    finish(1, e, c, 2 if (c, e) == (3, 1) else 1)
